import numpy as np
import ml_dtypes


def mxq(x, axis, fmt="e4m3"):
    dtype, down = {"e4m3": (ml_dtypes.float8_e4m3fn, 7), "e5m2": (ml_dtypes.float8_e5m2, 14)}[fmt]
    v = np.moveaxis(np.asarray(x, np.float32).astype(ml_dtypes.bfloat16).astype(np.float64), axis, -1)
    blocks = v.reshape(v.shape[:-1] + (-1, 32))
    amax = np.abs(blocks).max(-1, keepdims=True)
    byte = np.maximum(np.where(amax > 0, np.frexp(amax)[1] - 1 + 127, 0) - down, 1)
    scale = np.exp2(byte - 127.0)
    codes = (blocks / scale).astype(np.float32).astype(dtype).astype(np.float64)
    return np.moveaxis((codes * scale).reshape(v.shape), -1, axis)


WIDE = False


def mx_kscale(k):
    if not WIDE:
        return np.ones(k)
    levels = np.array([10, -10, 5, -5, 0])
    if k % 512:
        return np.exp2(np.random.permutation(np.resize(levels, k // 32))).repeat(32)
    a = np.empty((k // 512, 16))
    for p in range(k // 512):
        a[p, :8] = np.random.permutation(np.resize(levels, 8))
        for g in range(8):
            far = levels[np.abs(levels - a[p, g]) >= 10]
            a[p, g + 8] = far[np.random.randint(len(far))]
    return np.exp2(a.ravel()).repeat(32)


def f64(x):
    return np.asarray(x).astype(np.float64)


def striped(idx):
    return np.tile(idx.reshape(-1, 16).T, (8, 1)).astype(np.uint16)


def unstriped(offs):
    return offs[:16].T.reshape(-1).astype(np.int64)


def pack_weight(w):
    k, n = w.shape
    w = f64(np.asarray(w, np.float32).astype(ml_dtypes.bfloat16)).reshape(k // 32, 32, n)
    amax = np.abs(w).max(1)
    byte = np.clip(np.where(amax > 0, np.frexp(amax)[1] - 1 + 127 - 7, 1), 1, 254)
    scaled = (w * np.exp2(127.0 - byte)[:, None, :]).reshape(k, n).astype(np.float32)
    words = np.ascontiguousarray(scaled.reshape(k // 512, 128, 4, n).transpose(0, 1, 3, 2)).astype(ml_dtypes.float8_e4m3fn).view(np.uint8)
    return words, np.ascontiguousarray(byte.astype(np.uint8).reshape(k // 512, 16, n))


def unpack_weight(words, scales):
    g, p, n, _ = words.shape
    vals = np.ascontiguousarray(words).view(ml_dtypes.float8_e4m3fn).astype(np.float64) * np.repeat(np.exp2(scales.astype(np.float64) - 127.0), 8, axis=1)[..., None]
    return vals.transpose(0, 1, 3, 2).reshape(g * 512, n)


K, T, S, H, V, W, G = 512, 2048, 512, 512, 512, 1024, 2048
P = 2 ** 7


def setup_inputs():
    n = np.random.standard_normal
    s = mx_kscale(K)[:, None]
    u = mx_kscale(H)
    packed_xT = pack_weight(n((K, T)) * s)
    packed_eT = pack_weight(n((K, W)) * s)
    packed_vT = pack_weight(n((H, G)) / np.sqrt(H) / u[:, None])
    return {
        "x_words": packed_xT[0],
        "x_scales": packed_xT[1],
        "e_words": packed_eT[0],
        "e_scales": packed_eT[1],
        "w1": (n((K, H)) / np.sqrt(2 * K) / s * u).astype(np.float32),
        "w2": (n((K, H)) / np.sqrt(2 * K) / s * u).astype(np.float32),
        "v_words": packed_vT[0],
        "v_scales": packed_vT[1],
        "half": (np.tile(np.random.uniform(0.3, 1.0, G), (P, 1))).astype(np.float32),
        "offs": striped(np.random.permutation(T)[:S]),
        "code": striped(np.random.permutation(W)[:S]),
        "cand": striped(np.random.permutation(G)[:V]),
    }


def reference(x_words, x_scales, e_words, e_scales, w1, w2, v_words, v_scales, half, offs, code, cand):
    xq = unpack_weight(x_words, x_scales)[:, unstriped(offs)]
    e_code = unpack_weight(e_words, e_scales)[:, unstriped(code)]
    y = mxq(f64(w2), 0, "e4m3").T @ e_code
    rr = (mxq(f64(w1), 0, "e4m3").T @ xq) - y
    v_cand = unpack_weight(v_words, v_scales)[:, unstriped(cand)]
    z = (mxq(rr, 0, "e4m3").T @ v_cand) - (f64(half)[:1][:, unstriped(cand)])
    ex = np.exp(z - z.max(axis=1, keepdims=True))
    return ex / ex.sum(axis=1, keepdims=True)

@@ -1,0 +1,195 @@
+from contextlib import ExitStack
+
+import concourse.mybir as mybir
+from concourse.masks import make_identity
+
+F32 = mybir.dt.float32
+BF16 = mybir.dt.bfloat16
+I32 = mybir.dt.int32
+U32 = mybir.dt.uint32
+U16 = mybir.dt.uint16
+U8 = mybir.dt.uint8
+FP8X4 = mybir.dt.float8_e4m3fn_x4
+ACT = mybir.ActivationFunctionType
+ALU = mybir.AluOpType
+
+P = 128
+PACK = 4
+N = 512
+BLOCKS = N // P
+FLOPS = 3 * 2 * 512 * 512 * 512
+
+
+def tile_picked_yrvq_soft_p_kernel(
+    tc, x_words, x_scales, e_words, e_scales, w1, w2, v_words, v_scales, half, offs, code, cand, out
+):
+    nc = tc.nc
+    with ExitStack() as ctx:
+        sb = ctx.enter_context(tc.tile_pool(name="sb", bufs=1))
+        ps = ctx.enter_context(tc.psum_pool(name="ps", bufs=1))
+
+        def tile(shape, dtype, name):
+            return sb.tile(shape, dtype, name=name, align_bytes=64)
+
+        def load_list(src, name):
+            t = tile([P, N // 16], U16, name)
+            nc.sync.dma_start(t[:], src)
+            return t
+
+        def load_words(src, name):
+            t = tile([P, src.shape[2]], I32, name)
+            nc.sync.dma_start(t[:], src[0].rearrange("p n r -> p (n r)").bitcast(I32))
+            return t
+
+        def load_weight(src, name):
+            t = tile([P, PACK, N], F32, name)
+            nc.sync.dma_start(t[:], src.rearrange("(p j) c -> p j c", j=PACK))
+            return t
+
+        def clear_scales(src, name):
+            t = tile([P, src.shape[2]], U8, name)
+            nc.vector.memset(t[:].bitcast(I32), 0)
+            return t
+
+        def load_scales(t, src, k, queue):
+            for q in range(4):
+                queue.dma_start(
+                    t[32 * q + k : 32 * q + k + 4, :].bitcast(I32), src[0, 4 * q : 4 * q + 4, :].bitcast(I32)
+                )
+
+        def gather(dst, window, offsets, a, b):
+            nc.vector.tensor_copy(dst[:, a:b], window.indirect(offsets[:, a // 16 : b // 16]))
+
+        KX, KE, KV = 0, 4, 8
+
+        ident = tile([P, P], F32, "ident")
+        make_identity(nc, ident[:])
+
+        code_t = load_list(code, "code_t")
+        offs_t = load_list(offs, "offs_t")
+        cand_t = load_list(cand, "cand_t")
+        e_tab = load_words(e_words, "e_tab")
+        w2_raw = load_weight(w2, "w2_raw")
+
+        es_tab = clear_scales(e_scales, "es_tab")
+        xs_tab = clear_scales(x_scales, "xs_tab")
+        vs_tab = clear_scales(v_scales, "vs_tab")
+        load_scales(xs_tab, x_scales, KX, nc.scalar)
+        load_scales(es_tab, e_scales, KE, nc.gpsimd)
+        load_scales(vs_tab, v_scales, KV, nc.gpsimd)
+
+        warm = tile([P, 2], F32, "warm")
+        nc.vector.memset(warm[:, 0:1], 0.0)
+        nc.scalar.activation(warm[:, 1:2], warm[:, 0:1], ACT.Exp)
+
+        h_tab = tile([P, half.shape[1]], F32, "h_tab")
+        nc.vector.memset(h_tab[:, 0:2047], 0.0)
+        nc.vector.memset(h_tab[:, 2047:2048], 0.0)
+
+        w1_raw = load_weight(w1, "w1_raw")
+        x_tab = load_words(x_words, "x_tab")
+        v_tab = load_words(v_words, "v_tab")
+        nc.scalar.dma_start(h_tab[0:1, :], half[0:1, :])
+
+        def cast_weight(raw, name, sign):
+            g = tile([P, PACK, P, PACK], BF16, name)
+            nc.scalar.activation(
+                g[:].rearrange("p t m j -> p m j t"),
+                raw[:].rearrange("p j (m t) -> p m j t", t=PACK),
+                ACT.Copy,
+                scale=sign,
+            )
+            return g
+
+        def quantise(g, width, name):
+            c = tile([P, width], U32, name + "_c")
+            s = tile([P, width], U8, name + "_s")
+            nc.vector.quantize_mx(out=c[:].bitcast(FP8X4), scales=s[:], in_=g)
+            return c, s
+
+        e_g = tile([P, N], U32, "e_g")
+        x_g = tile([P, N], U32, "x_g")
+        v_g = tile([P, N], U32, "v_g")
+        es_g = tile([P, N], U8, "es_g")
+        xs_g = tile([P, N], U8, "xs_g")
+        vs_g = tile([P, N], U8, "vs_g")
+        h_g = tile([P, N], F32, "h_g")
+
+        w2_bf = cast_weight(w2_raw, "w2_bf", -1.0)
+        w1_bf = cast_weight(w1_raw, "w1_bf", 1.0)
+
+        gather(e_g, e_tab[:].bitcast(U32), code_t, 0, N)
+        gather(xs_g, xs_tab[:], offs_t, 0, N)
+        gather(es_g, es_tab[:], code_t, 0, N)
+        gather(h_g, h_tab[:], cand_t, 0, N)
+        w2_c, w2_s = quantise(w2_bf[:].rearrange("p t m j -> p (t m j)"), N, "w2")
+
+        rr_ps = [ps.tile([P, PACK, P], F32, name="rr_ps%d" % b) for b in range(BLOCKS)]
+
+        def project(b, w_c, w_s, a_g, a_s, k, first):
+            cols = slice(P * b, P * (b + 1))
+            for j in range(PACK):
+                js = slice(P * j, P * (j + 1))
+                nc.tensor.matmul_mx(
+                    out=rr_ps[b][:, j, :],
+                    lhsT=w_c[:, js].bitcast(FP8X4),
+                    lhsT_scale=w_s[:, js],
+                    rhs=a_g[:, cols].bitcast(FP8X4),
+                    rhs_scale=a_s[k:P, cols],
+                    start=(first and j == 0),
+                    stop=(not first and j == PACK - 1),
+                )
+
+        h_col_ps = ps.tile([P, BLOCKS, P], F32, name="h_col_ps", tag="z2")
+        for b in range(BLOCKS):
+            nc.tensor.transpose(h_col_ps[:, b, :], h_g[:, P * b : P * (b + 1)], ident[:])
+        h_col = tile([P, BLOCKS], F32, "h_col")
+        nc.scalar.copy(h_col[:], h_col_ps[:, :, 0])
+        h_row_ps = ps.tile([P, BLOCKS, P], F32, name="h_row_ps", tag="z3")
+        for b in range(BLOCKS):
+            nc.tensor.transpose(h_row_ps[:, b, :], h_col[:, b : b + 1].to_broadcast([P, P]), ident[:])
+        h_row = tile([P, N], F32, "h_row")
+        nc.scalar.copy(h_row[:], h_row_ps[:].rearrange("p b m -> p (b m)"))
+
+        for b in range(BLOCKS):
+            project(b, w2_c, w2_s, e_g, es_g, KE, True)
+
+        gather(vs_g, vs_tab[:], cand_t, 0, N)
+        gather(x_g, x_tab[:].bitcast(U32), offs_t, 0, N // 2)
+        w1_c, w1_s = quantise(w1_bf[:].rearrange("p t m j -> p (t m j)"), N, "w1")
+        gather(x_g, x_tab[:].bitcast(U32), offs_t, N // 2, N)
+        gather(v_g, v_tab[:].bitcast(U32), cand_t, 0, N)
+
+        rr_q = []
+        for b in range(BLOCKS):
+            project(b, w1_c, w1_s, x_g, xs_g, KX, False)
+            rr_bf = tile([P, P, PACK], BF16, "rr_bf%d" % b)
+            nc.scalar.copy(rr_bf[:], rr_ps[b][:].rearrange("p j t -> p t j"))
+            rr_q.append(quantise(rr_bf[:].rearrange("p t j -> p (t j)"), P, "rr%d" % b))
+
+        for b in range(BLOCKS):
+            z_ps = ps.tile([P, N], F32, name="z_ps%d" % b, tag="z%d" % b)
+            nc.tensor.matmul_mx(
+                out=z_ps[:],
+                lhsT=rr_q[b][0][:].bitcast(FP8X4),
+                lhsT_scale=rr_q[b][1][:],
+                rhs=v_g[:].bitcast(FP8X4),
+                rhs_scale=vs_g[KV:P, :],
+                start=True,
+                stop=True,
+            )
+            neg = tile([P, N], F32, "neg%d" % b)
+            nc.vector.tensor_tensor(neg[:], h_row[:], z_ps[:], ALU.subtract)
+            low = tile([P, 1], F32, "low%d" % b)
+            nc.vector.tensor_reduce(low[:], neg[:], mybir.AxisListType.X, ALU.min)
+            ex = tile([P, N], F32, "ex%d" % b)
+            total = tile([P, 1], F32, "total%d" % b)
+            nc.scalar.activation(ex[:], neg[:], ACT.Exp, bias=low[:], scale=-1.0, accum_out=total[:])
+            inv = tile([P, 1], F32, "inv%d" % b)
+            nc.vector.reciprocal(inv[:], total[:])
+            res = tile([P, N], F32, "res%d" % b)
+            if b < BLOCKS - 1:
+                nc.scalar.activation(res[:], ex[:], ACT.Copy, scale=inv[:])
+            else:
+                nc.vector.tensor_scalar(res[:], ex[:], inv[:], None, ALU.mult)
+            nc.sync.dma_start(out[P * b : P * (b + 1), :], res[:])

@@ -26,18 +26,22 @@ def tile_picked_yrvq_soft_p_kernel(
     nc = tc.nc
     with ExitStack() as ctx:
         sb = ctx.enter_context(tc.tile_pool(name="sb", bufs=1))
+        reuse = ctx.enter_context(tc.tile_pool(name="reuse", bufs=1))
         ps = ctx.enter_context(tc.psum_pool(name="ps", bufs=1))
 
         def tile(shape, dtype, name):
             return sb.tile(shape, dtype, name=name, align_bytes=64)
+
+        def placed(shape, dtype, name, offset):
+            return reuse.tile(shape, dtype, name=name, align_bytes=64, offset=offset)
 
         def load_list(src, name):
             t = tile([P, N // 16], U16, name)
             nc.sync.dma_start(t[:], src)
             return t
 
-        def load_words(src, name):
-            t = tile([P, src.shape[2]], I32, name)
+        def load_words(src, name, offset):
+            t = placed([P, src.shape[2]], I32, name, offset)
             nc.sync.dma_start(t[:], src[0].rearrange("p n r -> p (n r)").bitcast(I32))
             return t
 
@@ -48,7 +52,7 @@ def tile_picked_yrvq_soft_p_kernel(
 
         def clear_scales(src, name):
             t = tile([P, src.shape[2]], U8, name)
-            nc.vector.memset(t[:].bitcast(I32), 0)
+            nc.gpsimd.memset(t[:].bitcast(I32), 0)
             return t
 
         def load_scales(t, src, k, queue):
@@ -58,38 +62,38 @@ def tile_picked_yrvq_soft_p_kernel(
                 )
 
         def gather(dst, window, offsets, a, b):
-            nc.vector.tensor_copy(dst[:, a:b], window.indirect(offsets[:, a // 16 : b // 16]))
+            nc.vector.tensor_copy(dst[:], window.indirect(offsets[:, a // 16 : b // 16]))
 
         KX, KE, KV = 0, 4, 8
+        E_AT, H_AT, V_AT, X_AT = 0, 4096, 12288, 20480
 
-        ident = tile([P, P], F32, "ident")
-        make_identity(nc, ident[:])
 
         code_t = load_list(code, "code_t")
         offs_t = load_list(offs, "offs_t")
         cand_t = load_list(cand, "cand_t")
-        e_tab = load_words(e_words, "e_tab")
-        w2_raw = load_weight(w2, "w2_raw")
-
         es_tab = clear_scales(e_scales, "es_tab")
         xs_tab = clear_scales(x_scales, "xs_tab")
         vs_tab = clear_scales(v_scales, "vs_tab")
-        load_scales(xs_tab, x_scales, KX, nc.scalar)
-        load_scales(es_tab, e_scales, KE, nc.gpsimd)
-        load_scales(vs_tab, v_scales, KV, nc.gpsimd)
-
+        h_tab = placed([P, half.shape[1]], F32, "h_tab", H_AT)
+        nc.vector.memset(h_tab[:, 0:1399], 0.0)
+        nc.vector.memset(h_tab[:, 1399:1400], 0.0)
+        nc.gpsimd.memset(h_tab[:, 1400:2048], 0.0)
         warm = tile([P, 2], F32, "warm")
         nc.vector.memset(warm[:, 0:1], 0.0)
         nc.scalar.activation(warm[:, 1:2], warm[:, 0:1], ACT.Exp)
 
-        h_tab = tile([P, half.shape[1]], F32, "h_tab")
-        nc.vector.memset(h_tab[:, 0:2047], 0.0)
-        nc.vector.memset(h_tab[:, 2047:2048], 0.0)
-
+        load_scales(es_tab, e_scales, KE, nc.sync)
+        w2_raw = load_weight(w2, "w2_raw")
+        load_scales(xs_tab, x_scales, KX, nc.sync)
+        e_tab = load_words(e_words, "e_tab", E_AT)
         w1_raw = load_weight(w1, "w1_raw")
-        x_tab = load_words(x_words, "x_tab")
-        v_tab = load_words(v_words, "v_tab")
-        nc.scalar.dma_start(h_tab[0:1, :], half[0:1, :])
+        load_scales(vs_tab, v_scales, KV, nc.sync)
+        nc.sync.dma_start(h_tab[0:1, :], half[0:1, :])
+        x_tab = load_words(x_words, "x_tab", X_AT)
+        v_tab = load_words(v_words, "v_tab", V_AT)
+
+        ident = tile([P, P], F32, "ident")
+        make_identity(nc, ident[:])
 
         def cast_weight(raw, name, sign):
             g = tile([P, PACK, P, PACK], BF16, name)
@@ -101,28 +105,23 @@ def tile_picked_yrvq_soft_p_kernel(
             )
             return g
 
-        def quantise(g, width, name):
-            c = tile([P, width], U32, name + "_c")
+        def quantise(g, width, name, offset):
+            c = placed([P, width], U32, name + "_c", offset)
             s = tile([P, width], U8, name + "_s")
             nc.vector.quantize_mx(out=c[:].bitcast(FP8X4), scales=s[:], in_=g)
             return c, s
 
         e_g = tile([P, N], U32, "e_g")
-        x_g = tile([P, N], U32, "x_g")
-        v_g = tile([P, N], U32, "v_g")
         es_g = tile([P, N], U8, "es_g")
         xs_g = tile([P, N], U8, "xs_g")
-        vs_g = tile([P, N], U8, "vs_g")
-        h_g = tile([P, N], F32, "h_g")
 
         w2_bf = cast_weight(w2_raw, "w2_bf", -1.0)
         w1_bf = cast_weight(w1_raw, "w1_bf", 1.0)
 
-        gather(e_g, e_tab[:].bitcast(U32), code_t, 0, N)
-        gather(xs_g, xs_tab[:], offs_t, 0, N)
         gather(es_g, es_tab[:], code_t, 0, N)
-        gather(h_g, h_tab[:], cand_t, 0, N)
-        w2_c, w2_s = quantise(w2_bf[:].rearrange("p t m j -> p (t m j)"), N, "w2")
+        gather(xs_g, xs_tab[:], offs_t, 0, N)
+        gather(e_g, e_tab[:].bitcast(U32), code_t, 0, N)
+        w2_c, w2_s = quantise(w2_bf[:].rearrange("p t m j -> p (t m j)"), N, "w2", E_AT)
 
         rr_ps = [ps.tile([P, PACK, P], F32, name="rr_ps%d" % b) for b in range(BLOCKS)]
 
@@ -134,12 +133,19 @@ def tile_picked_yrvq_soft_p_kernel(
                     out=rr_ps[b][:, j, :],
                     lhsT=w_c[:, js].bitcast(FP8X4),
                     lhsT_scale=w_s[:, js],
-                    rhs=a_g[:, cols].bitcast(FP8X4),
+                    rhs=a_g.bitcast(FP8X4),
                     rhs_scale=a_s[k:P, cols],
                     start=(first and j == 0),
                     stop=(not first and j == PACK - 1),
                 )
 
+        for b in range(BLOCKS):
+            project(b, w2_c, w2_s, e_g[:, P * b : P * (b + 1)], es_g, KE, True)
+
+        vs_g = tile([P, N], U8, "vs_g")
+        gather(vs_g, vs_tab[:], cand_t, 0, N)
+        h_g = tile([P, N], F32, "h_g")
+        gather(h_g, h_tab[:], cand_t, 0, N)
         h_col_ps = ps.tile([P, BLOCKS, P], F32, name="h_col_ps", tag="z2")
         for b in range(BLOCKS):
             nc.tensor.transpose(h_col_ps[:, b, :], h_g[:, P * b : P * (b + 1)], ident[:])
@@ -151,21 +157,19 @@ def tile_picked_yrvq_soft_p_kernel(
         h_row = tile([P, N], F32, "h_row")
         nc.scalar.copy(h_row[:], h_row_ps[:].rearrange("p b m -> p (b m)"))
 
-        for b in range(BLOCKS):
-            project(b, w2_c, w2_s, e_g, es_g, KE, True)
-
-        gather(vs_g, vs_tab[:], cand_t, 0, N)
-        gather(x_g, x_tab[:].bitcast(U32), offs_t, 0, N // 2)
-        w1_c, w1_s = quantise(w1_bf[:].rearrange("p t m j -> p (t m j)"), N, "w1")
-        gather(x_g, x_tab[:].bitcast(U32), offs_t, N // 2, N)
+        x_g = [tile([P, N // 2], U32, "x_g0"), tile([P, N // 2], U32, "x_g1")]
+        w1_c, w1_s = quantise(w1_bf[:].rearrange("p t m j -> p (t m j)"), N, "w1", H_AT)
+        gather(x_g[0], x_tab[:].bitcast(U32), offs_t, 0, N // 2)
+        gather(x_g[1], x_tab[:].bitcast(U32), offs_t, N // 2, N)
+        v_g = tile([P, N], U32, "v_g")
         gather(v_g, v_tab[:].bitcast(U32), cand_t, 0, N)
 
         rr_q = []
         for b in range(BLOCKS):
-            project(b, w1_c, w1_s, x_g, xs_g, KX, False)
+            project(b, w1_c, w1_s, x_g[b // 2][:, P * (b % 2) : P * (b % 2 + 1)], xs_g, KX, False)
             rr_bf = tile([P, P, PACK], BF16, "rr_bf%d" % b)
             nc.scalar.copy(rr_bf[:], rr_ps[b][:].rearrange("p j t -> p t j"))
-            rr_q.append(quantise(rr_bf[:].rearrange("p t j -> p (t j)"), P, "rr%d" % b))
+            rr_q.append(quantise(rr_bf[:].rearrange("p t j -> p (t j)"), P, "rr%d" % b, V_AT + 512 * b))
 
         for b in range(BLOCKS):
             z_ps = ps.tile([P, N], F32, name="z_ps%d" % b, tag="z%d" % b)

@@ -55,11 +55,9 @@ def tile_picked_yrvq_soft_p_kernel(
             nc.gpsimd.memset(t[:].bitcast(I32), 0)
             return t
 
-        def load_scales(t, src, k, queue):
-            for q in range(4):
-                queue.dma_start(
-                    t[32 * q + k : 32 * q + k + 4, :].bitcast(I32), src[0, 4 * q : 4 * q + 4, :].bitcast(I32)
-                )
+        def load_scales(t, src, k, queues):
+            for r, queue in enumerate(queues):
+                queue.dma_start(t[k + r : P : 32, :].bitcast(I32), src[0, r:16:4, :].bitcast(I32))
 
         def gather(dst, window, offsets, a, b):
             nc.vector.tensor_copy(dst[:], window.indirect(offsets[:, a // 16 : b // 16]))
@@ -70,7 +68,6 @@ def tile_picked_yrvq_soft_p_kernel(
 
         code_t = load_list(code, "code_t")
         offs_t = load_list(offs, "offs_t")
-        cand_t = load_list(cand, "cand_t")
         es_tab = clear_scales(e_scales, "es_tab")
         xs_tab = clear_scales(x_scales, "xs_tab")
         vs_tab = clear_scales(v_scales, "vs_tab")
@@ -78,22 +75,22 @@ def tile_picked_yrvq_soft_p_kernel(
         nc.vector.memset(h_tab[:, 0:1399], 0.0)
         nc.vector.memset(h_tab[:, 1399:1400], 0.0)
         nc.gpsimd.memset(h_tab[:, 1400:2048], 0.0)
-        warm = tile([P, 2], F32, "warm")
-        nc.vector.memset(warm[:, 0:1], 0.0)
-        nc.scalar.activation(warm[:, 1:2], warm[:, 0:1], ACT.Exp)
 
-        load_scales(es_tab, e_scales, KE, nc.sync)
+        load_scales(es_tab, e_scales, KE, [nc.scalar] * 3 + [nc.sync])
         w2_raw = load_weight(w2, "w2_raw")
-        load_scales(xs_tab, x_scales, KX, nc.sync)
+        load_scales(xs_tab, x_scales, KX, [nc.sync] * 4)
         e_tab = load_words(e_words, "e_tab", E_AT)
         w1_raw = load_weight(w1, "w1_raw")
-        load_scales(vs_tab, v_scales, KV, nc.sync)
+        cand_t = load_list(cand, "cand_t")
+        load_scales(vs_tab, v_scales, KV, [nc.sync] * 4)
         nc.sync.dma_start(h_tab[0:1, :], half[0:1, :])
         x_tab = load_words(x_words, "x_tab", X_AT)
         v_tab = load_words(v_words, "v_tab", V_AT)
 
         ident = tile([P, P], F32, "ident")
         make_identity(nc, ident[:])
+        warm = tile([P, 1], F32, "warm")
+        nc.scalar.activation(warm[:], ident[:, 0:1], ACT.Exp)
 
         def cast_weight(raw, name, sign):
             g = tile([P, PACK, P, PACK], BF16, name)
@@ -165,18 +162,23 @@ def tile_picked_yrvq_soft_p_kernel(
         gather(v_g, v_tab[:].bitcast(U32), cand_t, 0, N)
 
         rr_q = []
-        for b in range(BLOCKS):
-            project(b, w1_c, w1_s, x_g[b // 2][:, P * (b % 2) : P * (b % 2 + 1)], xs_g, KX, False)
-            rr_bf = tile([P, P, PACK], BF16, "rr_bf%d" % b)
-            nc.scalar.copy(rr_bf[:], rr_ps[b][:].rearrange("p j t -> p t j"))
-            rr_q.append(quantise(rr_bf[:].rearrange("p t j -> p (t j)"), P, "rr%d" % b, V_AT + 512 * b))
+        for pair in range(BLOCKS // 2):
+            rr_bf = tile([P, 2 * P * PACK], BF16, "rr_bf%d" % pair)
+            for i in range(2):
+                b = 2 * pair + i
+                project(b, w1_c, w1_s, x_g[pair][:, P * i : P * (i + 1)], xs_g, KX, False)
+                nc.scalar.copy(
+                    rr_bf[:, N * i : N * (i + 1)].rearrange("p (t j) -> p t j", j=PACK),
+                    rr_ps[b][:].rearrange("p j t -> p t j"),
+                )
+            rr_q.append(quantise(rr_bf[:], 2 * P, "rr%d" % pair, V_AT + 1024 * pair))
 
         for b in range(BLOCKS):
             z_ps = ps.tile([P, N], F32, name="z_ps%d" % b, tag="z%d" % b)
             nc.tensor.matmul_mx(
                 out=z_ps[:],
-                lhsT=rr_q[b][0][:].bitcast(FP8X4),
-                lhsT_scale=rr_q[b][1][:],
+                lhsT=rr_q[b // 2][0][:, P * (b % 2) : P * (b % 2 + 1)].bitcast(FP8X4),
+                lhsT_scale=rr_q[b // 2][1][:, P * (b % 2) : P * (b % 2 + 1)],
                 rhs=v_g[:].bitcast(FP8X4),
                 rhs_scale=vs_g[KV:P, :],
                 start=True,
@@ -193,7 +195,7 @@ def tile_picked_yrvq_soft_p_kernel(
             nc.vector.reciprocal(inv[:], total[:])
             res = tile([P, N], F32, "res%d" % b)
             if b < BLOCKS - 1:
-                nc.scalar.activation(res[:], ex[:], ACT.Copy, scale=inv[:])
+                nc.gpsimd.tensor_scalar(res[:], ex[:], inv[:], 0.0, ALU.mult, ALU.add)
             else:
                 nc.vector.tensor_scalar(res[:], ex[:], inv[:], None, ALU.mult)
             nc.sync.dma_start(out[P * b : P * (b + 1), :], res[:])

@@ -19,6 +19,22 @@ N = 512
 BLOCKS = N // P
 FLOPS = 3 * 2 * 512 * 512 * 512
 
+X_ROW, E_ROW, V_ROW = 0, 4, 8
+
+E_AT = 0
+HALF_AT = E_AT + 1024 * 4
+V_AT = HALF_AT + 2048 * 4
+X_AT = V_AT + 2048 * 4
+ES_AT = X_AT + 2048 * 4
+XS_AT = ES_AT + 1024
+VS_AT = XS_AT + 2048
+W2_AT = VS_AT + 2048
+W1_AT = W2_AT + PACK * N * 4
+STAT_AT = W1_AT + PACK * N * 4
+STAT_BYTES = 64
+
+HALF_SPLIT = 1400
+
 
 def tile_picked_yrvq_soft_p_kernel(
     tc, x_words, x_scales, e_words, e_scales, w1, w2, v_words, v_scales, half, offs, code, cand, out
@@ -45,68 +61,67 @@ def tile_picked_yrvq_soft_p_kernel(
             nc.sync.dma_start(t[:], src[0].rearrange("p n r -> p (n r)").bitcast(I32))
             return t
 
-        def load_weight(src, name):
-            t = tile([P, PACK, N], F32, name)
+        def load_weight(src, name, offset):
+            t = placed([P, PACK, N], F32, name, offset)
             nc.sync.dma_start(t[:], src.rearrange("(p j) c -> p j c", j=PACK))
             return t
 
-        def clear_scales(src, name):
-            t = tile([P, src.shape[2]], U8, name)
+        def clear_scales(src, name, offset):
+            t = placed([P, src.shape[2]], U8, name, offset)
             nc.gpsimd.memset(t[:].bitcast(I32), 0)
             return t
 
-        def load_scales(t, src, k, queues):
-            for r, queue in enumerate(queues):
-                queue.dma_start(t[k + r : P : 32, :].bitcast(I32), src[0, r:16:4, :].bitcast(I32))
+        def load_scales(t, src, first_row):
+            for r in range(4):
+                nc.sync.dma_start(t[first_row + r : P : 32, :].bitcast(I32), src[0, r:16:4, :].bitcast(I32))
 
         def gather(dst, window, offsets, a, b):
             nc.vector.tensor_copy(dst[:], window.indirect(offsets[:, a // 16 : b // 16]))
 
-        KX, KE, KV = 0, 4, 8
-        E_AT, H_AT, V_AT, X_AT = 0, 4096, 12288, 20480
-
-
         code_t = load_list(code, "code_t")
         offs_t = load_list(offs, "offs_t")
-        es_tab = clear_scales(e_scales, "es_tab")
-        xs_tab = clear_scales(x_scales, "xs_tab")
-        vs_tab = clear_scales(v_scales, "vs_tab")
-        h_tab = placed([P, half.shape[1]], F32, "h_tab", H_AT)
-        nc.vector.memset(h_tab[:, 0:1399], 0.0)
-        nc.vector.memset(h_tab[:, 1399:1400], 0.0)
-        nc.gpsimd.memset(h_tab[:, 1400:2048], 0.0)
-
-        load_scales(es_tab, e_scales, KE, [nc.scalar] * 3 + [nc.sync])
-        w2_raw = load_weight(w2, "w2_raw")
-        load_scales(xs_tab, x_scales, KX, [nc.sync] * 4)
-        e_tab = load_words(e_words, "e_tab", E_AT)
-        w1_raw = load_weight(w1, "w1_raw")
         cand_t = load_list(cand, "cand_t")
-        load_scales(vs_tab, v_scales, KV, [nc.sync] * 4)
-        nc.sync.dma_start(h_tab[0:1, :], half[0:1, :])
+        es_tab = clear_scales(e_scales, "es_tab", ES_AT)
+        xs_tab = clear_scales(x_scales, "xs_tab", XS_AT)
+        vs_tab = clear_scales(v_scales, "vs_tab", VS_AT)
+
+        half_tab = placed([P, half.shape[1]], F32, "half_tab", HALF_AT)
+        nc.vector.memset(half_tab[:, 0 : HALF_SPLIT - 1], 0.0)
+        nc.vector.memset(half_tab[:, HALF_SPLIT - 1 : HALF_SPLIT], 0.0)
+        nc.gpsimd.memset(half_tab[:, HALF_SPLIT : half.shape[1]], 0.0)
+
+        load_scales(es_tab, e_scales, E_ROW)
+        w2_raw = load_weight(w2, "w2_raw", W2_AT)
+        load_scales(xs_tab, x_scales, X_ROW)
+        nc.sync.dma_start(half_tab[0:1, :], half[0:1, :])
+        e_tab = load_words(e_words, "e_tab", E_AT)
+        w1_raw = load_weight(w1, "w1_raw", W1_AT)
+        load_scales(vs_tab, v_scales, V_ROW)
         x_tab = load_words(x_words, "x_tab", X_AT)
         v_tab = load_words(v_words, "v_tab", V_AT)
 
         ident = tile([P, P], F32, "ident")
         make_identity(nc, ident[:])
-        warm = tile([P, 1], F32, "warm")
-        nc.scalar.activation(warm[:], ident[:, 0:1], ACT.Exp)
+
+        preload = tile([P, 1], F32, "preload")
+        nc.scalar.activation(preload[:], ident[:, 0:1], ACT.Exp)
 
         def cast_weight(raw, name, sign):
             g = tile([P, PACK, P, PACK], BF16, name)
-            nc.scalar.activation(
-                g[:].rearrange("p t m j -> p m j t"),
-                raw[:].rearrange("p j (m t) -> p m j t", t=PACK),
-                ACT.Copy,
-                scale=sign,
-            )
+            for t0 in (0, 2):
+                nc.scalar.activation(
+                    g[:, t0 : t0 + 2].rearrange("p t m j -> p m j t"),
+                    raw[:].rearrange("p j (m t) -> p m j t", t=PACK)[:, :, :, t0 : t0 + 2],
+                    ACT.Copy,
+                    scale=sign,
+                )
             return g
 
-        def quantise(g, width, name, offset):
-            c = placed([P, width], U32, name + "_c", offset)
-            s = tile([P, width], U8, name + "_s")
-            nc.vector.quantize_mx(out=c[:].bitcast(FP8X4), scales=s[:], in_=g)
-            return c, s
+        def quantise(values, width, name, offset):
+            words = placed([P, width], U32, name + "_words", offset)
+            scales = tile([P, width], U8, name + "_scales")
+            nc.vector.quantize_mx(out=words[:].bitcast(FP8X4), scales=scales[:], in_=values)
+            return words, scales
 
         e_g = tile([P, N], U32, "e_g")
         es_g = tile([P, N], U8, "es_g")
@@ -117,85 +132,128 @@ def tile_picked_yrvq_soft_p_kernel(
 
         gather(es_g, es_tab[:], code_t, 0, N)
         gather(xs_g, xs_tab[:], offs_t, 0, N)
+        half_g = tile([P, N], F32, "half_g")
+        gather(half_g, half_tab[:], cand_t, 0, N)
         gather(e_g, e_tab[:].bitcast(U32), code_t, 0, N)
-        w2_c, w2_s = quantise(w2_bf[:].rearrange("p t m j -> p (t m j)"), N, "w2", E_AT)
+        w2_words, w2_scales = quantise(w2_bf[:].rearrange("p t m j -> p (t m j)"), N, "w2", E_AT)
 
-        rr_ps = [ps.tile([P, PACK, P], F32, name="rr_ps%d" % b) for b in range(BLOCKS)]
+        rr_ps = [ps.tile([P, PACK, P], F32, name="rr_ps%d" % b, tag="r%d" % b) for b in range(BLOCKS)]
 
-        def project(b, w_c, w_s, a_g, a_s, k, first):
-            cols = slice(P * b, P * (b + 1))
+        def project(b, w_words, w_scales, picked, picked_scales, first_row, opens):
             for j in range(PACK):
                 js = slice(P * j, P * (j + 1))
                 nc.tensor.matmul_mx(
                     out=rr_ps[b][:, j, :],
-                    lhsT=w_c[:, js].bitcast(FP8X4),
-                    lhsT_scale=w_s[:, js],
-                    rhs=a_g.bitcast(FP8X4),
-                    rhs_scale=a_s[k:P, cols],
-                    start=(first and j == 0),
-                    stop=(not first and j == PACK - 1),
+                    lhsT=w_words[:, js].bitcast(FP8X4),
+                    lhsT_scale=w_scales[:, js],
+                    rhs=picked.bitcast(FP8X4),
+                    rhs_scale=picked_scales[first_row:P, P * b : P * (b + 1)],
+                    start=(opens and j == 0),
+                    stop=(not opens and j == PACK - 1),
                 )
 
         for b in range(BLOCKS):
-            project(b, w2_c, w2_s, e_g[:, P * b : P * (b + 1)], es_g, KE, True)
+            project(b, w2_words, w2_scales, e_g[:, P * b : P * (b + 1)], es_g, E_ROW, True)
 
         vs_g = tile([P, N], U8, "vs_g")
         gather(vs_g, vs_tab[:], cand_t, 0, N)
-        h_g = tile([P, N], F32, "h_g")
-        gather(h_g, h_tab[:], cand_t, 0, N)
-        h_col_ps = ps.tile([P, BLOCKS, P], F32, name="h_col_ps", tag="z2")
-        for b in range(BLOCKS):
-            nc.tensor.transpose(h_col_ps[:, b, :], h_g[:, P * b : P * (b + 1)], ident[:])
-        h_col = tile([P, BLOCKS], F32, "h_col")
-        nc.scalar.copy(h_col[:], h_col_ps[:, :, 0])
-        h_row_ps = ps.tile([P, BLOCKS, P], F32, name="h_row_ps", tag="z3")
-        for b in range(BLOCKS):
-            nc.tensor.transpose(h_row_ps[:, b, :], h_col[:, b : b + 1].to_broadcast([P, P]), ident[:])
-        h_row = tile([P, N], F32, "h_row")
-        nc.scalar.copy(h_row[:], h_row_ps[:].rearrange("p b m -> p (b m)"))
+
+        half_col_ps = ps.tile([P, BLOCKS, P], F32, name="half_col_ps", tag="z2")
+        for c in range(BLOCKS):
+            nc.tensor.transpose(half_col_ps[:, c, :], half_g[:, P * c : P * (c + 1)], ident[:])
+        half_col = placed([P, BLOCKS], F32, "half_col", W1_AT)
+        nc.scalar.copy(half_col[:], half_col_ps[:, :, 0])
+        half_row_ps = ps.tile([P, BLOCKS, P], F32, name="half_row_ps", tag="z3")
+        for c in range(BLOCKS):
+            nc.tensor.transpose(half_row_ps[:, c, :], half_col[:, c : c + 1].to_broadcast([P, P]), ident[:])
+        half_row = tile([P, N], F32, "half_row")
+        nc.scalar.copy(half_row[:], half_row_ps[:].rearrange("p c m -> p (c m)"))
 
         x_g = [tile([P, N // 2], U32, "x_g0"), tile([P, N // 2], U32, "x_g1")]
-        w1_c, w1_s = quantise(w1_bf[:].rearrange("p t m j -> p (t m j)"), N, "w1", H_AT)
+        w1_words, w1_scales = quantise(w1_bf[:].rearrange("p t m j -> p (t m j)"), N, "w1", VS_AT)
         gather(x_g[0], x_tab[:].bitcast(U32), offs_t, 0, N // 2)
         gather(x_g[1], x_tab[:].bitcast(U32), offs_t, N // 2, N)
         v_g = tile([P, N], U32, "v_g")
         gather(v_g, v_tab[:].bitcast(U32), cand_t, 0, N)
 
         rr_q = []
-        for pair in range(BLOCKS // 2):
-            rr_bf = tile([P, 2 * P * PACK], BF16, "rr_bf%d" % pair)
-            for i in range(2):
-                b = 2 * pair + i
-                project(b, w1_c, w1_s, x_g[pair][:, P * i : P * (i + 1)], xs_g, KX, False)
+        for group in ((0,), (1,), (2, 3)):
+            rr_bf = tile([P, len(group) * N], BF16, "rr_bf%d" % group[0])
+            for i, b in enumerate(group):
+                project(b, w1_words, w1_scales, x_g[b // 2][:, P * (b % 2) : P * (b % 2 + 1)], xs_g, X_ROW, False)
                 nc.scalar.copy(
                     rr_bf[:, N * i : N * (i + 1)].rearrange("p (t j) -> p t j", j=PACK),
                     rr_ps[b][:].rearrange("p j t -> p t j"),
                 )
-            rr_q.append(quantise(rr_bf[:], 2 * P, "rr%d" % pair, V_AT + 1024 * pair))
+            rr_q.append(quantise(rr_bf[:], len(group) * P, "rr%d" % group[0], V_AT + 4 * P * group[0]))
 
-        for b in range(BLOCKS):
+        neg = [None] * BLOCKS
+        low = [None] * BLOCKS
+
+        def score_rows(b):
             z_ps = ps.tile([P, N], F32, name="z_ps%d" % b, tag="z%d" % b)
             nc.tensor.matmul_mx(
                 out=z_ps[:],
-                lhsT=rr_q[b // 2][0][:, P * (b % 2) : P * (b % 2 + 1)].bitcast(FP8X4),
-                lhsT_scale=rr_q[b // 2][1][:, P * (b % 2) : P * (b % 2 + 1)],
+                lhsT=rr_q[b][0][:].bitcast(FP8X4),
+                lhsT_scale=rr_q[b][1][:],
                 rhs=v_g[:].bitcast(FP8X4),
-                rhs_scale=vs_g[KV:P, :],
+                rhs_scale=vs_g[V_ROW:P, :],
                 start=True,
                 stop=True,
             )
-            neg = tile([P, N], F32, "neg%d" % b)
-            nc.vector.tensor_tensor(neg[:], h_row[:], z_ps[:], ALU.subtract)
-            low = tile([P, 1], F32, "low%d" % b)
-            nc.vector.tensor_reduce(low[:], neg[:], mybir.AxisListType.X, ALU.min)
+            neg[b] = tile([P, N], F32, "neg%d" % b)
+            nc.vector.tensor_tensor(neg[b][:], half_row[:], z_ps[:], ALU.subtract)
+
+        def score_columns():
+            neg_t = []
+            for pair in range(BLOCKS // 2):
+                zt_ps = ps.tile([P, 2, 2 * P], F32, name="zt_ps%d" % pair, tag="z%d" % (2 + pair))
+                for i in range(2):
+                    cs = slice(P * (2 * pair + i), P * (2 * pair + i + 1))
+                    nc.tensor.matmul_mx(
+                        out=zt_ps[:, i, :],
+                        lhsT=v_g[:, cs].bitcast(FP8X4),
+                        lhsT_scale=vs_g[V_ROW:P, cs],
+                        rhs=rr_q[2][0][:].bitcast(FP8X4),
+                        rhs_scale=rr_q[2][1][:],
+                        start=True,
+                        stop=True,
+                    )
+                for i in range(2):
+                    c = 2 * pair + i
+                    t = tile([P, 2 * P], F32, "neg_t%d" % c)
+                    nc.scalar.activation(t[:], zt_ps[:, i, :], ACT.Identity, bias=half_col[:, c : c + 1], scale=-1.0)
+                    neg_t.append(t)
+            for i in range(2):
+                neg[2 + i] = ps.tile([P, N], F32, name="neg%d" % (2 + i), tag="r%d" % i)
+            for c in range(BLOCKS):
+                for i in range(2):
+                    nc.tensor.transpose(neg[2 + i][:, P * c : P * (c + 1)], neg_t[c][:, P * i : P * (i + 1)], ident[:])
+
+        def row_min(b):
+            low[b] = placed([P, 1], F32, "low%d" % b, STAT_AT + STAT_BYTES * b)
+            nc.vector.tensor_reduce(low[b][:], neg[b][:], mybir.AxisListType.X, ALU.min)
+
+        def finish(b):
             ex = tile([P, N], F32, "ex%d" % b)
-            total = tile([P, 1], F32, "total%d" % b)
-            nc.scalar.activation(ex[:], neg[:], ACT.Exp, bias=low[:], scale=-1.0, accum_out=total[:])
+            total = placed([P, 1], F32, "total%d" % b, STAT_AT + STAT_BYTES * (2 if b == 0 else BLOCKS + b))
+            nc.scalar.activation(ex[:], neg[b][:], ACT.Exp, bias=low[b][:], scale=-1.0, accum_out=total[:])
             inv = tile([P, 1], F32, "inv%d" % b)
             nc.vector.reciprocal(inv[:], total[:])
             res = tile([P, N], F32, "res%d" % b)
-            if b < BLOCKS - 1:
+            if b == 0:
                 nc.gpsimd.tensor_scalar(res[:], ex[:], inv[:], 0.0, ALU.mult, ALU.add)
             else:
                 nc.vector.tensor_scalar(res[:], ex[:], inv[:], None, ALU.mult)
             nc.sync.dma_start(out[P * b : P * (b + 1), :], res[:])
+
+        score_rows(0)
+        score_rows(1)
+        score_columns()
+        row_min(0)
+        row_min(1)
+        finish(0)
+        row_min(2)
+        row_min(3)
+        for b in range(1, BLOCKS):
+            finish(b)

from contextlib import ExitStack

import concourse.mybir as mybir
from concourse.masks import make_identity

F32 = mybir.dt.float32
BF16 = mybir.dt.bfloat16
I32 = mybir.dt.int32
U32 = mybir.dt.uint32
U16 = mybir.dt.uint16
U8 = mybir.dt.uint8
FP8X4 = mybir.dt.float8_e4m3fn_x4
ACT = mybir.ActivationFunctionType
ALU = mybir.AluOpType

P = 128
PACK = 4
N = 512
BLOCKS = N // P
FLOPS = 3 * 2 * 512 * 512 * 512

X_ROW, E_ROW, V_ROW = 0, 4, 8

E_AT = 0
HALF_AT = E_AT + 1024 * 4
V_AT = HALF_AT + 2048 * 4
X_AT = V_AT + 2048 * 4
ES_AT = X_AT + 2048 * 4
XS_AT = ES_AT + 1024
VS_AT = XS_AT + 2048
W2_AT = VS_AT + 2048
W1_AT = W2_AT + PACK * N * 4
STAT_AT = W1_AT + PACK * N * 4
STAT_BYTES = 64

HALF_SPLIT = 1400


def tile_picked_yrvq_soft_p_kernel(
    tc, x_words, x_scales, e_words, e_scales, w1, w2, v_words, v_scales, half, offs, code, cand, out
):
    nc = tc.nc
    with ExitStack() as ctx:
        sb = ctx.enter_context(tc.tile_pool(name="sb", bufs=1))
        reuse = ctx.enter_context(tc.tile_pool(name="reuse", bufs=1))
        ps = ctx.enter_context(tc.psum_pool(name="ps", bufs=1))

        def tile(shape, dtype, name):
            return sb.tile(shape, dtype, name=name, align_bytes=64)

        def placed(shape, dtype, name, offset):
            return reuse.tile(shape, dtype, name=name, align_bytes=64, offset=offset)

        def load_list(src, name):
            t = tile([P, N // 16], U16, name)
            nc.sync.dma_start(t[:], src)
            return t

        def load_words(src, name, offset):
            t = placed([P, src.shape[2]], I32, name, offset)
            nc.sync.dma_start(t[:], src[0].rearrange("p n r -> p (n r)").bitcast(I32))
            return t

        def load_weight(src, name, offset):
            t = placed([P, PACK, N], F32, name, offset)
            nc.sync.dma_start(t[:], src.rearrange("(p j) c -> p j c", j=PACK))
            return t

        def clear_scales(src, name, offset):
            t = placed([P, src.shape[2]], U8, name, offset)
            nc.gpsimd.memset(t[:].bitcast(I32), 0)
            return t

        def load_scales(t, src, first_row):
            for r in range(4):
                nc.sync.dma_start(t[first_row + r : P : 32, :].bitcast(I32), src[0, r:16:4, :].bitcast(I32))

        def gather(dst, window, offsets, a, b):
            nc.vector.tensor_copy(dst[:], window.indirect(offsets[:, a // 16 : b // 16]))

        code_t = load_list(code, "code_t")
        offs_t = load_list(offs, "offs_t")
        cand_t = load_list(cand, "cand_t")
        es_tab = clear_scales(e_scales, "es_tab", ES_AT)
        xs_tab = clear_scales(x_scales, "xs_tab", XS_AT)
        vs_tab = clear_scales(v_scales, "vs_tab", VS_AT)

        half_tab = placed([P, half.shape[1]], F32, "half_tab", HALF_AT)
        nc.vector.memset(half_tab[:, 0 : HALF_SPLIT - 1], 0.0)
        nc.vector.memset(half_tab[:, HALF_SPLIT - 1 : HALF_SPLIT], 0.0)
        nc.gpsimd.memset(half_tab[:, HALF_SPLIT : half.shape[1]], 0.0)

        load_scales(es_tab, e_scales, E_ROW)
        w2_raw = load_weight(w2, "w2_raw", W2_AT)
        load_scales(xs_tab, x_scales, X_ROW)
        nc.sync.dma_start(half_tab[0:1, :], half[0:1, :])
        e_tab = load_words(e_words, "e_tab", E_AT)
        w1_raw = load_weight(w1, "w1_raw", W1_AT)
        load_scales(vs_tab, v_scales, V_ROW)
        x_tab = load_words(x_words, "x_tab", X_AT)
        v_tab = load_words(v_words, "v_tab", V_AT)

        ident = tile([P, P], F32, "ident")
        make_identity(nc, ident[:])

        preload = tile([P, 1], F32, "preload")
        nc.scalar.activation(preload[:], ident[:, 0:1], ACT.Exp)

        def cast_weight(raw, name, sign):
            g = tile([P, PACK, P, PACK], BF16, name)
            for t0 in (0, 2):
                nc.scalar.activation(
                    g[:, t0 : t0 + 2].rearrange("p t m j -> p m j t"),
                    raw[:].rearrange("p j (m t) -> p m j t", t=PACK)[:, :, :, t0 : t0 + 2],
                    ACT.Copy,
                    scale=sign,
                )
            return g

        def quantise(values, width, name, offset):
            words = placed([P, width], U32, name + "_words", offset)
            scales = tile([P, width], U8, name + "_scales")
            nc.vector.quantize_mx(out=words[:].bitcast(FP8X4), scales=scales[:], in_=values)
            return words, scales

        e_g = tile([P, N], U32, "e_g")
        es_g = tile([P, N], U8, "es_g")
        xs_g = tile([P, N], U8, "xs_g")

        w2_bf = cast_weight(w2_raw, "w2_bf", -1.0)
        w1_bf = cast_weight(w1_raw, "w1_bf", 1.0)

        gather(es_g, es_tab[:], code_t, 0, N)
        gather(xs_g, xs_tab[:], offs_t, 0, N)
        half_g = tile([P, N], F32, "half_g")
        gather(half_g, half_tab[:], cand_t, 0, N)
        gather(e_g, e_tab[:].bitcast(U32), code_t, 0, N)
        w2_words, w2_scales = quantise(w2_bf[:].rearrange("p t m j -> p (t m j)"), N, "w2", E_AT)

        rr_ps = [ps.tile([P, PACK, P], F32, name="rr_ps%d" % b, tag="r%d" % b) for b in range(BLOCKS)]

        def project(b, w_words, w_scales, picked, picked_scales, first_row, opens):
            for j in range(PACK):
                js = slice(P * j, P * (j + 1))
                nc.tensor.matmul_mx(
                    out=rr_ps[b][:, j, :],
                    lhsT=w_words[:, js].bitcast(FP8X4),
                    lhsT_scale=w_scales[:, js],
                    rhs=picked.bitcast(FP8X4),
                    rhs_scale=picked_scales[first_row:P, P * b : P * (b + 1)],
                    start=(opens and j == 0),
                    stop=(not opens and j == PACK - 1),
                )

        for b in range(BLOCKS):
            project(b, w2_words, w2_scales, e_g[:, P * b : P * (b + 1)], es_g, E_ROW, True)

        vs_g = tile([P, N], U8, "vs_g")
        gather(vs_g, vs_tab[:], cand_t, 0, N)

        half_col_ps = ps.tile([P, BLOCKS, P], F32, name="half_col_ps", tag="z2")
        for c in range(BLOCKS):
            nc.tensor.transpose(half_col_ps[:, c, :], half_g[:, P * c : P * (c + 1)], ident[:])
        half_col = placed([P, BLOCKS], F32, "half_col", W1_AT)
        nc.scalar.copy(half_col[:], half_col_ps[:, :, 0])
        half_row_ps = ps.tile([P, BLOCKS, P], F32, name="half_row_ps", tag="z3")
        for c in range(BLOCKS):
            nc.tensor.transpose(half_row_ps[:, c, :], half_col[:, c : c + 1].to_broadcast([P, P]), ident[:])
        half_row = tile([P, N], F32, "half_row")
        nc.scalar.copy(half_row[:], half_row_ps[:].rearrange("p c m -> p (c m)"))

        x_g = [tile([P, N // 2], U32, "x_g0"), tile([P, N // 2], U32, "x_g1")]
        w1_words, w1_scales = quantise(w1_bf[:].rearrange("p t m j -> p (t m j)"), N, "w1", VS_AT)
        gather(x_g[0], x_tab[:].bitcast(U32), offs_t, 0, N // 2)
        gather(x_g[1], x_tab[:].bitcast(U32), offs_t, N // 2, N)
        v_g = tile([P, N], U32, "v_g")
        gather(v_g, v_tab[:].bitcast(U32), cand_t, 0, N)

        rr_q = []
        for group in ((0,), (1,), (2, 3)):
            rr_bf = tile([P, len(group) * N], BF16, "rr_bf%d" % group[0])
            for i, b in enumerate(group):
                project(b, w1_words, w1_scales, x_g[b // 2][:, P * (b % 2) : P * (b % 2 + 1)], xs_g, X_ROW, False)
                nc.scalar.copy(
                    rr_bf[:, N * i : N * (i + 1)].rearrange("p (t j) -> p t j", j=PACK),
                    rr_ps[b][:].rearrange("p j t -> p t j"),
                )
            rr_q.append(quantise(rr_bf[:], len(group) * P, "rr%d" % group[0], V_AT + 4 * P * group[0]))

        neg = [None] * BLOCKS
        low = [None] * BLOCKS

        def score_rows(b):
            z_ps = ps.tile([P, N], F32, name="z_ps%d" % b, tag="z%d" % b)
            nc.tensor.matmul_mx(
                out=z_ps[:],
                lhsT=rr_q[b][0][:].bitcast(FP8X4),
                lhsT_scale=rr_q[b][1][:],
                rhs=v_g[:].bitcast(FP8X4),
                rhs_scale=vs_g[V_ROW:P, :],
                start=True,
                stop=True,
            )
            neg[b] = tile([P, N], F32, "neg%d" % b)
            nc.vector.tensor_tensor(neg[b][:], half_row[:], z_ps[:], ALU.subtract)

        def score_columns():
            neg_t = []
            for pair in range(BLOCKS // 2):
                zt_ps = ps.tile([P, 2, 2 * P], F32, name="zt_ps%d" % pair, tag="z%d" % (2 + pair))
                for i in range(2):
                    cs = slice(P * (2 * pair + i), P * (2 * pair + i + 1))
                    nc.tensor.matmul_mx(
                        out=zt_ps[:, i, :],
                        lhsT=v_g[:, cs].bitcast(FP8X4),
                        lhsT_scale=vs_g[V_ROW:P, cs],
                        rhs=rr_q[2][0][:].bitcast(FP8X4),
                        rhs_scale=rr_q[2][1][:],
                        start=True,
                        stop=True,
                    )
                for i in range(2):
                    c = 2 * pair + i
                    t = tile([P, 2 * P], F32, "neg_t%d" % c)
                    nc.scalar.activation(t[:], zt_ps[:, i, :], ACT.Identity, bias=half_col[:, c : c + 1], scale=-1.0)
                    neg_t.append(t)
            for i in range(2):
                neg[2 + i] = ps.tile([P, N], F32, name="neg%d" % (2 + i), tag="r%d" % i)
            for c in range(BLOCKS):
                for i in range(2):
                    nc.tensor.transpose(neg[2 + i][:, P * c : P * (c + 1)], neg_t[c][:, P * i : P * (i + 1)], ident[:])

        def row_min(b):
            low[b] = placed([P, 1], F32, "low%d" % b, STAT_AT + STAT_BYTES * b)
            nc.vector.tensor_reduce(low[b][:], neg[b][:], mybir.AxisListType.X, ALU.min)

        def finish(b):
            ex = tile([P, N], F32, "ex%d" % b)
            total = placed([P, 1], F32, "total%d" % b, STAT_AT + STAT_BYTES * (2 if b == 0 else BLOCKS + b))
            nc.scalar.activation(ex[:], neg[b][:], ACT.Exp, bias=low[b][:], scale=-1.0, accum_out=total[:])
            inv = tile([P, 1], F32, "inv%d" % b)
            nc.vector.reciprocal(inv[:], total[:])
            res = tile([P, N], F32, "res%d" % b)
            if b == 0:
                nc.gpsimd.tensor_scalar(res[:], ex[:], inv[:], 0.0, ALU.mult, ALU.add)
            else:
                nc.vector.tensor_scalar(res[:], ex[:], inv[:], None, ALU.mult)
            nc.sync.dma_start(out[P * b : P * (b + 1), :], res[:])

        score_rows(0)
        score_rows(1)
        score_columns()
        row_min(0)
        row_min(1)
        finish(0)
        row_min(2)
        row_min(3)
        for b in range(1, BLOCKS):
            finish(b)
